import numpy as np
import ml_dtypes


def mxq(x, axis, fmt="e4m3"):
    dtype, down = {"e4m3": (ml_dtypes.float8_e4m3fn, 7), "e5m2": (ml_dtypes.float8_e5m2, 14)}[fmt]
    v = np.moveaxis(np.asarray(x, np.float32).astype(ml_dtypes.bfloat16).astype(np.float64), axis, -1)
    blocks = v.reshape(v.shape[:-1] + (-1, 32))
    amax = np.abs(blocks).max(-1, keepdims=True)
    byte = np.maximum(np.where(amax > 0, np.frexp(amax)[1] - 1 + 127, 0) - down, 1)
    scale = np.exp2(byte - 127.0)
    codes = (blocks / scale).astype(np.float32).astype(dtype).astype(np.float64)
    return np.moveaxis((codes * scale).reshape(v.shape), -1, axis)


WIDE = False


def mx_kscale(k):
    if not WIDE:
        return np.ones(k)
    levels = np.array([10, -10, 5, -5, 0])
    if k % 512:
        return np.exp2(np.random.permutation(np.resize(levels, k // 32))).repeat(32)
    a = np.empty((k // 512, 16))
    for p in range(k // 512):
        a[p, :8] = np.random.permutation(np.resize(levels, 8))
        for g in range(8):
            far = levels[np.abs(levels - a[p, g]) >= 10]
            a[p, g + 8] = far[np.random.randint(len(far))]
    return np.exp2(a.ravel()).repeat(32)


def f64(x):
    return np.asarray(x).astype(np.float64)


E2M1 = np.array([0.0, 0.5, 1.0, 1.5, 2.0, 3.0, 4.0, 6.0, -0.0, -0.5, -1.0, -1.5, -2.0, -3.0, -4.0, -6.0])


def pack_weight(w, fmt):
    k, n = w.shape
    w = f64(np.asarray(w, np.float32).astype(ml_dtypes.bfloat16)).reshape(k // 32, 32, n)
    amax = np.abs(w).max(1)
    if fmt == "e4m3":
        byte = np.frexp(amax)[1] - 1 + 127 - 7
    else:
        mant, ex = np.frexp(amax / 6.0)
        byte = np.where(mant > 0.5, ex, ex - 1) + 127
    byte = np.clip(np.where(amax > 0, byte, 1), 1, 254)
    scaled = (w * np.exp2(127.0 - byte)[:, None, :]).reshape(k, n).astype(np.float32)
    by_word = np.ascontiguousarray(scaled.reshape(k // 512, 128, 4, n).transpose(0, 1, 3, 2))
    if fmt == "e4m3":
        words = by_word.astype(ml_dtypes.float8_e4m3fn).view(np.uint8)
    else:
        c = by_word.astype(ml_dtypes.float4_e2m1fn).view(np.uint8) & 0xF
        words = (c[..., 0::2] | (c[..., 1::2] << 4)).reshape(k // 512, 128, 2 * n)
    return np.ascontiguousarray(words), np.ascontiguousarray(byte.astype(np.uint8).reshape(k // 512, 16, n))


def unpack_weight(words, scales, fmt):
    g, _, n = scales.shape
    words = np.ascontiguousarray(words).reshape(g, 128, n, -1)
    if fmt == "e4m3":
        vals = words.view(ml_dtypes.float8_e4m3fn).astype(np.float64)
    else:
        nib = np.empty((g, 128, n, 4), np.uint8)
        nib[..., 0::2] = words & 0xF
        nib[..., 1::2] = words >> 4
        vals = E2M1[nib]
    vals = vals * np.repeat(np.exp2(scales.astype(np.float64) - 127.0), 8, axis=1)[..., None]
    return vals.transpose(0, 1, 3, 2).reshape(g * 512, n)


K, M, T = 1536, 1024, 1536


def setup_inputs():
    n = np.random.standard_normal
    s = mx_kscale(K)[:, None]
    x = n((K, T)) * s
    x4 = pack_weight(x, "e2m1")
    rest = x - unpack_weight(*x4, "e2m1")
    p_w4 = pack_weight(n((K, M)) / np.sqrt(K) / s, "e2m1")
    return {
        "x4_words": x4[0],
        "x4_scales": x4[1],
        "xr": (rest).astype(np.float32),
        "w4_words": p_w4[0],
        "w4_scales": p_w4[1],
        "g": (n((1024, 1536))).astype(np.float32),
    }


def reference(x4_words, x4_scales, xr, w4_words, w4_scales, g):
    x4_ = unpack_weight(x4_words, x4_scales, "e2m1")
    xr_ = mxq(f64(xr), 0, "e4m3")
    w4_ = unpack_weight(w4_words, w4_scales, "e2m1")
    y = w4_.T @ x4_ + w4_.T @ xr_
    return f64(g) * y

@@ -1,0 +1,198 @@
+from contextlib import ExitStack
+
+import concourse.mybir as mybir
+
+K, M, T = 1536, 1024, 1536
+FLOPS = 4 * K * M * T
+
+F32 = mybir.dt.float32
+BF16 = mybir.dt.bfloat16
+I32 = mybir.dt.int32
+U32 = mybir.dt.uint32
+U8 = mybir.dt.uint8
+FP8X4 = mybir.dt.float8_e4m3fn_x4
+FP4X4 = mybir.dt.float4_e2m1fn_x4
+
+P = 128
+PACK = 4
+K_PASS = P * PACK
+A = K // K_PASS
+MT = M // P
+TB = 512
+NB = T // TB
+V_COLS = 320
+
+
+def tile_mix_xres_fm_mul_kernel(tc, x4_words, x4_scales, xr, w4_words, w4_scales, g, out):
+    nc = tc.nc
+    with ExitStack() as ctx:
+        keep = ctx.enter_context(tc.tile_pool(name="keep", bufs=1))
+        stage = ctx.enter_context(tc.tile_pool(name="stage", bufs=3))
+        psum = ctx.enter_context(tc.psum_pool(name="psum", bufs=1))
+        ctx.enter_context(tc.manual_schedule())
+
+        w_words = keep.tile([P, A, 2 * M], U8, name="w_words", align_bytes=64)
+        x_words = keep.tile([P, A, 2 * T], U8, name="x_words", align_bytes=64)
+        w_plane = keep.tile([P, A, M], U8, name="w_plane", align_bytes=64)
+        x_plane = keep.tile([P, A, T], U8, name="x_plane", align_bytes=64)
+        warm = keep.tile([P, 8], F32, name="warm")
+
+        nc.vector.memset(warm[:], 0.0)
+        nc.vector.memset(w_plane[:].rearrange("p a n -> p (a n)").bitcast(I32), 0)
+        nc.vector.memset(x_plane[:].rearrange("p a n -> p (a n)").bitcast(I32), 0)
+
+        nc.sync.dma_start(out=w_words[:].bitcast(I32), in_=w4_words.rearrange("a p b -> p a b").bitcast(I32))
+        nc.sync.dma_start(out=x_words[:].bitcast(I32), in_=x4_words.rearrange("a p b -> p a b").bitcast(I32))
+
+        raw_first = {}
+        raw_rest = {}
+
+        def load_xr(a, first):
+            rows = xr[a * K_PASS : (a + 1) * K_PASS, :].rearrange("(p j) t -> p j t", j=PACK)
+            if first:
+                raw = keep.tile([P, PACK, TB], F32, name="raw_first%d" % a)
+                nc.sync.dma_start(out=raw[:], in_=rows[:, :, 0:TB])
+                raw_first[a] = raw
+            else:
+                raw = keep.tile([P, PACK, T - TB], F32, name="raw_rest%d" % a)
+                nc.sync.dma_start(out=raw[:], in_=rows[:, :, TB:T])
+                raw_rest[a] = raw
+
+        w_rows = w4_scales.rearrange("a (q r) n -> r q a n", r=4)
+        x_rows = x4_scales.rearrange("a (q r) n -> r q a n", r=4)
+        for r in range(4):
+            nc.scalar.dma_start(out=w_plane[r : P : 32, :, :].bitcast(I32), in_=w_rows[r].bitcast(I32))
+        for r in range(4):
+            queue = nc.scalar if r < 2 else nc.gpsimd
+            queue.dma_start(out=x_plane[r : P : 32, :, :].bitcast(I32), in_=x_rows[r].bitcast(I32))
+        for first in (True, False):
+            for a in range(A):
+                load_xr(a, first)
+        g_tiles = []
+        for h in range(MT // 2):
+            gt = keep.tile([P, 2, T], F32, name="g%d" % h)
+            nc.sync.dma_start(
+                out=gt[:], in_=g[h * 2 * P : (h + 1) * 2 * P, :].rearrange("(i p) t -> p i t", p=P)
+            )
+            g_tiles.append(gt)
+
+        nc.scalar.copy(out=warm[:, 0:1], in_=warm[:, 4:5])
+
+        codes = {}
+        scales = {}
+
+        def quantise(a, b):
+            if b == 0:
+                raw = raw_first[a][:]
+            else:
+                raw = raw_rest[a][:, :, (b - 1) * TB : b * TB]
+            grouped = stage.tile([P, TB, PACK], BF16, name="grouped", align_bytes=64)
+            nc.vector.tensor_copy(
+                out=grouped[:, 0:V_COLS, :], in_=raw[:, :, 0:V_COLS].rearrange("p j t -> p t j")
+            )
+            nc.scalar.copy(
+                out=grouped[:, V_COLS:TB, :], in_=raw[:, :, V_COLS:TB].rearrange("p j t -> p t j")
+            )
+            code = keep.tile([P, TB], U32, name="code%d_%d" % (a, b), align_bytes=64)
+            scale = keep.tile([P, TB], U8, name="scale%d_%d" % (a, b), align_bytes=64)
+            nc.vector.quantize_mx(
+                out=code[:].bitcast(FP8X4),
+                scales=scale[:],
+                in_=grouped[:].rearrange("p t j -> p (t j)"),
+            )
+            codes[a, b] = code
+            scales[a, b] = scale
+
+        banks = {}
+
+        def open_bank(i):
+            banks[i] = psum.tile([P, TB], F32, name="bank%d" % i)
+
+        def x4_pass(i, a, m, b):
+            nc.tensor.matmul_mx(
+                out=banks[i][:],
+                lhsT=w_words[:, a, 2 * m * P : 2 * (m + 1) * P].bitcast(FP4X4),
+                lhsT_scale=w_plane[:, a, m * P : (m + 1) * P],
+                rhs=x_words[:, a, 2 * b * TB : 2 * (b + 1) * TB].bitcast(FP4X4),
+                rhs_scale=x_plane[:, a, b * TB : (b + 1) * TB],
+                start=(a == 0),
+                stop=False,
+            )
+
+        def xr_pass(i, a, m, b):
+            nc.tensor.matmul_mx(
+                out=banks[i][:],
+                lhsT=w_words[:, a, 2 * m * P : 2 * (m + 1) * P].bitcast(FP4X4),
+                lhsT_scale=w_plane[:, a, m * P : (m + 1) * P],
+                rhs=codes[a, b][:].bitcast(FP8X4),
+                rhs_scale=scales[a, b][:],
+                start=False,
+                stop=(a == A - 1),
+            )
+
+        y_first = {}
+
+        def empty_first(m):
+            y = keep.tile([P, TB], F32, name="y%d" % m)
+            if m % 2 == 0:
+                nc.scalar.copy(out=y[:], in_=banks[m][:])
+            else:
+                nc.vector.tensor_copy(out=y[:], in_=banks[m][:])
+            y_first[m] = y
+
+        def g_cols(m, b):
+            return g_tiles[m // 2][:, m % 2, b * TB : (b + 1) * TB]
+
+        def finish(i, m, b):
+            gm = g_cols(m, b)
+            nc.vector.tensor_mul(out=gm, in0=banks[i][:], in1=gm)
+
+        def finish_first(m):
+            gm = g_cols(m, 0)
+            nc.vector.tensor_mul(out=gm, in0=y_first[m][:], in1=gm)
+
+        def store(m):
+            nc.sync.dma_start(out=out[m * P : (m + 1) * P, :], in_=g_tiles[m // 2][:, m % 2, :])
+
+        for m in range(MT):
+            open_bank(m)
+        for a in range(A):
+            for m in range(MT):
+                x4_pass(m, a, m, 0)
+        for a in range(A):
+            quantise(a, 0)
+            for m in range(MT):
+                xr_pass(m, a, m, 0)
+        quantise(0, 1)
+        quantise(0, 2)
+        half = [(m, b) for m in range(MT // 2) for b in (1, 2)]
+        for i, (m, b) in enumerate(half):
+            empty_first(i)
+            open_bank(i)
+            for a in range(A):
+                x4_pass(i, a, m, b)
+        quantise(1, 1)
+        quantise(1, 2)
+        quantise(2, 1)
+        quantise(2, 2)
+        for a in range(A):
+            for i, (m, b) in enumerate(half):
+                xr_pass(i, a, m, b)
+        for i, (m, b) in enumerate(half):
+            if b == 1:
+                finish_first(m)
+            finish(i, m, b)
+            if b == 2:
+                store(m)
+        for i, (m, b) in enumerate(half):
+            m = m + MT // 2
+            open_bank(i)
+            for a in range(A):
+                x4_pass(i, a, m, b)
+            for a in range(A):
+                xr_pass(i, a, m, b)
+            if b == 1:
+                finish_first(m)
+            finish(i, m, b)
+            if b == 2:
+                store(m)

@@ -37,37 +37,32 @@ def tile_mix_xres_fm_mul_kernel(tc, x4_words, x4_scales, xr, w4_words, w4_scales
         x_plane = keep.tile([P, A, T], U8, name="x_plane", align_bytes=64)
         warm = keep.tile([P, 8], F32, name="warm")
 
-        nc.vector.memset(warm[:], 0.0)
         nc.vector.memset(w_plane[:].rearrange("p a n -> p (a n)").bitcast(I32), 0)
         nc.vector.memset(x_plane[:].rearrange("p a n -> p (a n)").bitcast(I32), 0)
-
-        nc.sync.dma_start(out=w_words[:].bitcast(I32), in_=w4_words.rearrange("a p b -> p a b").bitcast(I32))
-        nc.sync.dma_start(out=x_words[:].bitcast(I32), in_=x4_words.rearrange("a p b -> p a b").bitcast(I32))
-
-        raw_first = {}
-        raw_rest = {}
-
-        def load_xr(a, first):
-            rows = xr[a * K_PASS : (a + 1) * K_PASS, :].rearrange("(p j) t -> p j t", j=PACK)
-            if first:
-                raw = keep.tile([P, PACK, TB], F32, name="raw_first%d" % a)
-                nc.sync.dma_start(out=raw[:], in_=rows[:, :, 0:TB])
-                raw_first[a] = raw
-            else:
-                raw = keep.tile([P, PACK, T - TB], F32, name="raw_rest%d" % a)
-                nc.sync.dma_start(out=raw[:], in_=rows[:, :, TB:T])
-                raw_rest[a] = raw
+        nc.vector.memset(warm[:], 0.0)
 
         w_rows = w4_scales.rearrange("a (q r) n -> r q a n", r=4)
         x_rows = x4_scales.rearrange("a (q r) n -> r q a n", r=4)
+        nc.sync.dma_start(out=w_words[:].bitcast(I32), in_=w4_words.rearrange("a p b -> p a b").bitcast(I32))
         for r in range(4):
-            nc.scalar.dma_start(out=w_plane[r : P : 32, :, :].bitcast(I32), in_=w_rows[r].bitcast(I32))
+            nc.sync.dma_start(out=w_plane[r : P : 32, :, :].bitcast(I32), in_=w_rows[r].bitcast(I32))
+        nc.sync.dma_start(out=x_words[:].bitcast(I32), in_=x4_words.rearrange("a p b -> p a b").bitcast(I32))
         for r in range(4):
-            queue = nc.scalar if r < 2 else nc.gpsimd
-            queue.dma_start(out=x_plane[r : P : 32, :, :].bitcast(I32), in_=x_rows[r].bitcast(I32))
-        for first in (True, False):
-            for a in range(A):
-                load_xr(a, first)
+            nc.sync.dma_start(out=x_plane[r : P : 32, :, :].bitcast(I32), in_=x_rows[r].bitcast(I32))
+
+        raw = {}
+
+        def load_xr(a, c0, c1):
+            rows = xr[a * K_PASS : (a + 1) * K_PASS, :].rearrange("(p j) t -> p j t", j=PACK)
+            piece = keep.tile([P, PACK, c1 - c0], F32, name="raw%d_%d" % (a, c0))
+            nc.sync.dma_start(out=piece[:], in_=rows[:, :, c0:c1])
+            for b in range(c0 // TB, c1 // TB):
+                raw[a, b] = piece[:, :, b * TB - c0 : (b + 1) * TB - c0]
+
+        for a in range(A):
+            load_xr(a, 0, TB)
+        for a in range(A):
+            load_xr(a, TB, T)
         g_tiles = []
         for h in range(MT // 2):
             gt = keep.tile([P, 2, T], F32, name="g%d" % h)
@@ -82,16 +77,13 @@ def tile_mix_xres_fm_mul_kernel(tc, x4_words, x4_scales, xr, w4_words, w4_scales
         scales = {}
 
         def quantise(a, b):
-            if b == 0:
-                raw = raw_first[a][:]
-            else:
-                raw = raw_rest[a][:, :, (b - 1) * TB : b * TB]
+            rows = raw[a, b]
             grouped = stage.tile([P, TB, PACK], BF16, name="grouped", align_bytes=64)
             nc.vector.tensor_copy(
-                out=grouped[:, 0:V_COLS, :], in_=raw[:, :, 0:V_COLS].rearrange("p j t -> p t j")
+                out=grouped[:, 0:V_COLS, :], in_=rows[:, :, 0:V_COLS].rearrange("p j t -> p t j")
             )
             nc.scalar.copy(
-                out=grouped[:, V_COLS:TB, :], in_=raw[:, :, V_COLS:TB].rearrange("p j t -> p t j")
+                out=grouped[:, V_COLS:TB, :], in_=rows[:, :, V_COLS:TB].rearrange("p j t -> p t j")
             )
             code = keep.tile([P, TB], U32, name="code%d_%d" % (a, b), align_bytes=64)
             scale = keep.tile([P, TB], U8, name="scale%d_%d" % (a, b), align_bytes=64)
@@ -152,7 +144,8 @@ def tile_mix_xres_fm_mul_kernel(tc, x4_words, x4_scales, xr, w4_words, w4_scales
             nc.vector.tensor_mul(out=gm, in0=y_first[m][:], in1=gm)
 
         def store(m):
-            nc.sync.dma_start(out=out[m * P : (m + 1) * P, :], in_=g_tiles[m // 2][:, m % 2, :])
+            queue = nc.sync if m % 2 == 0 else nc.scalar
+            queue.dma_start(out=out[m * P : (m + 1) * P, :], in_=g_tiles[m // 2][:, m % 2, :])
 
         for m in range(MT):
             open_bank(m)

@@ -20,7 +20,7 @@ A = K // K_PASS
 MT = M // P
 TB = 512
 NB = T // TB
-V_COLS = 320
+V_COLS = 256
 
 
 def tile_mix_xres_fm_mul_kernel(tc, x4_words, x4_scales, xr, w4_words, w4_scales, g, out):
@@ -31,10 +31,11 @@ def tile_mix_xres_fm_mul_kernel(tc, x4_words, x4_scales, xr, w4_words, w4_scales
         psum = ctx.enter_context(tc.psum_pool(name="psum", bufs=1))
         ctx.enter_context(tc.manual_schedule())
 
-        w_words = keep.tile([P, A, 2 * M], U8, name="w_words", align_bytes=64)
-        x_words = keep.tile([P, A, 2 * T], U8, name="x_words", align_bytes=64)
-        w_plane = keep.tile([P, A, M], U8, name="w_plane", align_bytes=64)
-        x_plane = keep.tile([P, A, T], U8, name="x_plane", align_bytes=64)
+        w_words = keep.tile([P, A, 2 * M], U8, name="w_words", align_bytes=256)
+        x_first = keep.tile([P, A, 2 * TB], U8, name="x_first", align_bytes=256)
+        x_rest = keep.tile([P, A, 2 * (T - TB)], U8, name="x_rest", align_bytes=256)
+        w_plane = keep.tile([P, A, M], U8, name="w_plane", align_bytes=256)
+        x_plane = keep.tile([P, A, T], U8, name="x_plane", align_bytes=256)
         warm = keep.tile([P, 8], F32, name="warm")
 
         nc.vector.memset(w_plane[:].rearrange("p a n -> p (a n)").bitcast(I32), 0)
@@ -43,26 +44,30 @@ def tile_mix_xres_fm_mul_kernel(tc, x4_words, x4_scales, xr, w4_words, w4_scales
 
         w_rows = w4_scales.rearrange("a (q r) n -> r q a n", r=4)
         x_rows = x4_scales.rearrange("a (q r) n -> r q a n", r=4)
-        nc.sync.dma_start(out=w_words[:].bitcast(I32), in_=w4_words.rearrange("a p b -> p a b").bitcast(I32))
-        for r in range(4):
-            nc.sync.dma_start(out=w_plane[r : P : 32, :, :].bitcast(I32), in_=w_rows[r].bitcast(I32))
-        nc.sync.dma_start(out=x_words[:].bitcast(I32), in_=x4_words.rearrange("a p b -> p a b").bitcast(I32))
-        for r in range(4):
-            nc.sync.dma_start(out=x_plane[r : P : 32, :, :].bitcast(I32), in_=x_rows[r].bitcast(I32))
-
+        x_src = x4_words.rearrange("a p b -> p a b")
+        w_src = w4_words.rearrange("a p b -> p a b")
         raw = {}
 
-        def load_xr(a, c0, c1):
+        def load_xr(queue, a, c0, c1):
             rows = xr[a * K_PASS : (a + 1) * K_PASS, :].rearrange("(p j) t -> p j t", j=PACK)
             piece = keep.tile([P, PACK, c1 - c0], F32, name="raw%d_%d" % (a, c0))
-            nc.sync.dma_start(out=piece[:], in_=rows[:, :, c0:c1])
+            queue.dma_start(out=piece[:], in_=rows[:, :, c0:c1])
             for b in range(c0 // TB, c1 // TB):
                 raw[a, b] = piece[:, :, b * TB - c0 : (b + 1) * TB - c0]
 
+        nc.gpsimd.dma_start(out=x_first[:].bitcast(I32), in_=x_src[:, :, 0 : 2 * TB].bitcast(I32))
+        load_xr(nc.gpsimd, 0, 0, TB)
+        nc.sync.dma_start(out=w_words[:, 0:1, :].bitcast(I32), in_=w_src[:, 0:1, :].bitcast(I32))
+        for r in range(4):
+            nc.sync.dma_start(out=w_plane[r : P : 32, :, :].bitcast(I32), in_=w_rows[r].bitcast(I32))
+        for r in range(4):
+            nc.sync.dma_start(out=x_plane[r : P : 32, :, :].bitcast(I32), in_=x_rows[r].bitcast(I32))
+        nc.sync.dma_start(out=w_words[:, 1:A, :].bitcast(I32), in_=w_src[:, 1:A, :].bitcast(I32))
+        load_xr(nc.sync, 1, 0, TB)
+        load_xr(nc.sync, 2, 0, TB)
+        nc.sync.dma_start(out=x_rest[:].bitcast(I32), in_=x_src[:, :, 2 * TB : 2 * T].bitcast(I32))
         for a in range(A):
-            load_xr(a, 0, TB)
-        for a in range(A):
-            load_xr(a, TB, T)
+            load_xr(nc.sync, a, TB, T)
         g_tiles = []
         for h in range(MT // 2):
             gt = keep.tile([P, 2, T], F32, name="g%d" % h)
@@ -78,15 +83,15 @@ def tile_mix_xres_fm_mul_kernel(tc, x4_words, x4_scales, xr, w4_words, w4_scales
 
         def quantise(a, b):
             rows = raw[a, b]
-            grouped = stage.tile([P, TB, PACK], BF16, name="grouped", align_bytes=64)
+            grouped = stage.tile([P, TB, PACK], BF16, name="grouped", align_bytes=256)
             nc.vector.tensor_copy(
                 out=grouped[:, 0:V_COLS, :], in_=rows[:, :, 0:V_COLS].rearrange("p j t -> p t j")
             )
             nc.scalar.copy(
                 out=grouped[:, V_COLS:TB, :], in_=rows[:, :, V_COLS:TB].rearrange("p j t -> p t j")
             )
-            code = keep.tile([P, TB], U32, name="code%d_%d" % (a, b), align_bytes=64)
-            scale = keep.tile([P, TB], U8, name="scale%d_%d" % (a, b), align_bytes=64)
+            code = keep.tile([P, TB], U32, name="code%d_%d" % (a, b), align_bytes=256)
+            scale = keep.tile([P, TB], U8, name="scale%d_%d" % (a, b), align_bytes=256)
             nc.vector.quantize_mx(
                 out=code[:].bitcast(FP8X4),
                 scales=scale[:],
@@ -101,11 +106,13 @@ def tile_mix_xres_fm_mul_kernel(tc, x4_words, x4_scales, xr, w4_words, w4_scales
             banks[i] = psum.tile([P, TB], F32, name="bank%d" % i)
 
         def x4_pass(i, a, m, b):
+            words = x_first if b == 0 else x_rest
+            b0 = b if b == 0 else b - 1
             nc.tensor.matmul_mx(
                 out=banks[i][:],
                 lhsT=w_words[:, a, 2 * m * P : 2 * (m + 1) * P].bitcast(FP4X4),
                 lhsT_scale=w_plane[:, a, m * P : (m + 1) * P],
-                rhs=x_words[:, a, 2 * b * TB : 2 * (b + 1) * TB].bitcast(FP4X4),
+                rhs=words[:, a, 2 * b0 * TB : 2 * (b0 + 1) * TB].bitcast(FP4X4),
                 rhs_scale=x_plane[:, a, b * TB : (b + 1) * TB],
                 start=(a == 0),
                 stop=False,
@@ -122,30 +129,21 @@ def tile_mix_xres_fm_mul_kernel(tc, x4_words, x4_scales, xr, w4_words, w4_scales
                 stop=(a == A - 1),
             )
 
-        y_first = {}
+        held = {}
 
-        def empty_first(m):
-            y = keep.tile([P, TB], F32, name="y%d" % m)
-            if m % 2 == 0:
-                nc.scalar.copy(out=y[:], in_=banks[m][:])
-            else:
-                nc.vector.tensor_copy(out=y[:], in_=banks[m][:])
-            y_first[m] = y
-
-        def g_cols(m, b):
-            return g_tiles[m // 2][:, m % 2, b * TB : (b + 1) * TB]
+        def hold(engine_copy, i, m, b):
+            y = keep.tile([P, TB], F32, name="y%d_%d" % (m, b))
+            engine_copy(out=y[:], in_=banks[i][:])
+            held[m, b] = y
 
         def finish(i, m, b):
-            gm = g_cols(m, b)
-            nc.vector.tensor_mul(out=gm, in0=banks[i][:], in1=gm)
+            gm = g_tiles[m // 2][:, m % 2, b * TB : (b + 1) * TB]
+            y = held[m, b] if (m, b) in held else banks[i]
+            nc.vector.tensor_mul(out=gm, in0=y[:], in1=gm)
 
-        def finish_first(m):
-            gm = g_cols(m, 0)
-            nc.vector.tensor_mul(out=gm, in0=y_first[m][:], in1=gm)
-
-        def store(m):
+        def store(m, c0, c1):
             queue = nc.sync if m % 2 == 0 else nc.scalar
-            queue.dma_start(out=out[m * P : (m + 1) * P, :], in_=g_tiles[m // 2][:, m % 2, :])
+            queue.dma_start(out=out[m * P : (m + 1) * P, c0:c1], in_=g_tiles[m // 2][:, m % 2, c0:c1])
 
         for m in range(MT):
             open_bank(m)
@@ -156,36 +154,32 @@ def tile_mix_xres_fm_mul_kernel(tc, x4_words, x4_scales, xr, w4_words, w4_scales
             quantise(a, 0)
             for m in range(MT):
                 xr_pass(m, a, m, 0)
-        quantise(0, 1)
-        quantise(0, 2)
         half = [(m, b) for m in range(MT // 2) for b in (1, 2)]
         for i, (m, b) in enumerate(half):
-            empty_first(i)
+            hold(nc.scalar.copy if i % 2 == 0 else nc.vector.tensor_copy, i, i, 0)
             open_bank(i)
             for a in range(A):
                 x4_pass(i, a, m, b)
-        quantise(1, 1)
-        quantise(1, 2)
+        for a in (0, 1):
+            quantise(a, 1)
+            quantise(a, 2)
         quantise(2, 1)
         quantise(2, 2)
         for a in range(A):
             for i, (m, b) in enumerate(half):
                 xr_pass(i, a, m, b)
         for i, (m, b) in enumerate(half):
-            if b == 1:
-                finish_first(m)
-            finish(i, m, b)
-            if b == 2:
-                store(m)
-        for i, (m, b) in enumerate(half):
-            m = m + MT // 2
+            hold(nc.scalar.copy, i, m, b)
             open_bank(i)
             for a in range(A):
-                x4_pass(i, a, m, b)
+                x4_pass(i, a, m + MT // 2, b)
             for a in range(A):
-                xr_pass(i, a, m, b)
-            if b == 1:
-                finish_first(m)
-            finish(i, m, b)
-            if b == 2:
-                store(m)
+                xr_pass(i, a, m + MT // 2, b)
+        for m in range(MT):
+            finish(0, m, 0)
+            for b in (1, 2):
+                finish(2 * (m % (MT // 2)) + b - 1, m, b)
+                if m == MT - 1:
+                    store(m, (b - 1) * 2 * TB, (b + 1) * TB)
+            if m < MT - 1:
+                store(m, 0, T)

from contextlib import ExitStack

import concourse.mybir as mybir

K, M, T = 1536, 1024, 1536
FLOPS = 4 * K * M * T

F32 = mybir.dt.float32
BF16 = mybir.dt.bfloat16
I32 = mybir.dt.int32
U32 = mybir.dt.uint32
U8 = mybir.dt.uint8
FP8X4 = mybir.dt.float8_e4m3fn_x4
FP4X4 = mybir.dt.float4_e2m1fn_x4

P = 128
PACK = 4
K_PASS = P * PACK
A = K // K_PASS
MT = M // P
TB = 512
NB = T // TB
V_COLS = 256


def tile_mix_xres_fm_mul_kernel(tc, x4_words, x4_scales, xr, w4_words, w4_scales, g, out):
    nc = tc.nc
    with ExitStack() as ctx:
        keep = ctx.enter_context(tc.tile_pool(name="keep", bufs=1))
        stage = ctx.enter_context(tc.tile_pool(name="stage", bufs=3))
        psum = ctx.enter_context(tc.psum_pool(name="psum", bufs=1))
        ctx.enter_context(tc.manual_schedule())

        w_words = keep.tile([P, A, 2 * M], U8, name="w_words", align_bytes=256)
        x_first = keep.tile([P, A, 2 * TB], U8, name="x_first", align_bytes=256)
        x_rest = keep.tile([P, A, 2 * (T - TB)], U8, name="x_rest", align_bytes=256)
        w_plane = keep.tile([P, A, M], U8, name="w_plane", align_bytes=256)
        x_plane = keep.tile([P, A, T], U8, name="x_plane", align_bytes=256)
        warm = keep.tile([P, 8], F32, name="warm")

        nc.vector.memset(w_plane[:].rearrange("p a n -> p (a n)").bitcast(I32), 0)
        nc.vector.memset(x_plane[:].rearrange("p a n -> p (a n)").bitcast(I32), 0)
        nc.vector.memset(warm[:], 0.0)

        w_rows = w4_scales.rearrange("a (q r) n -> r q a n", r=4)
        x_rows = x4_scales.rearrange("a (q r) n -> r q a n", r=4)
        x_src = x4_words.rearrange("a p b -> p a b")
        w_src = w4_words.rearrange("a p b -> p a b")
        raw = {}

        def load_xr(queue, a, c0, c1):
            rows = xr[a * K_PASS : (a + 1) * K_PASS, :].rearrange("(p j) t -> p j t", j=PACK)
            piece = keep.tile([P, PACK, c1 - c0], F32, name="raw%d_%d" % (a, c0))
            queue.dma_start(out=piece[:], in_=rows[:, :, c0:c1])
            for b in range(c0 // TB, c1 // TB):
                raw[a, b] = piece[:, :, b * TB - c0 : (b + 1) * TB - c0]

        nc.gpsimd.dma_start(out=x_first[:].bitcast(I32), in_=x_src[:, :, 0 : 2 * TB].bitcast(I32))
        load_xr(nc.gpsimd, 0, 0, TB)
        nc.sync.dma_start(out=w_words[:, 0:1, :].bitcast(I32), in_=w_src[:, 0:1, :].bitcast(I32))
        for r in range(4):
            nc.sync.dma_start(out=w_plane[r : P : 32, :, :].bitcast(I32), in_=w_rows[r].bitcast(I32))
        for r in range(4):
            nc.sync.dma_start(out=x_plane[r : P : 32, :, :].bitcast(I32), in_=x_rows[r].bitcast(I32))
        nc.sync.dma_start(out=w_words[:, 1:A, :].bitcast(I32), in_=w_src[:, 1:A, :].bitcast(I32))
        load_xr(nc.sync, 1, 0, TB)
        load_xr(nc.sync, 2, 0, TB)
        nc.sync.dma_start(out=x_rest[:].bitcast(I32), in_=x_src[:, :, 2 * TB : 2 * T].bitcast(I32))
        for a in range(A):
            load_xr(nc.sync, a, TB, T)
        g_tiles = []
        for h in range(MT // 2):
            gt = keep.tile([P, 2, T], F32, name="g%d" % h)
            nc.sync.dma_start(
                out=gt[:], in_=g[h * 2 * P : (h + 1) * 2 * P, :].rearrange("(i p) t -> p i t", p=P)
            )
            g_tiles.append(gt)

        nc.scalar.copy(out=warm[:, 0:1], in_=warm[:, 4:5])

        codes = {}
        scales = {}

        def quantise(a, b):
            rows = raw[a, b]
            grouped = stage.tile([P, TB, PACK], BF16, name="grouped", align_bytes=256)
            nc.vector.tensor_copy(
                out=grouped[:, 0:V_COLS, :], in_=rows[:, :, 0:V_COLS].rearrange("p j t -> p t j")
            )
            nc.scalar.copy(
                out=grouped[:, V_COLS:TB, :], in_=rows[:, :, V_COLS:TB].rearrange("p j t -> p t j")
            )
            code = keep.tile([P, TB], U32, name="code%d_%d" % (a, b), align_bytes=256)
            scale = keep.tile([P, TB], U8, name="scale%d_%d" % (a, b), align_bytes=256)
            nc.vector.quantize_mx(
                out=code[:].bitcast(FP8X4),
                scales=scale[:],
                in_=grouped[:].rearrange("p t j -> p (t j)"),
            )
            codes[a, b] = code
            scales[a, b] = scale

        banks = {}

        def open_bank(i):
            banks[i] = psum.tile([P, TB], F32, name="bank%d" % i)

        def x4_pass(i, a, m, b):
            words = x_first if b == 0 else x_rest
            b0 = b if b == 0 else b - 1
            nc.tensor.matmul_mx(
                out=banks[i][:],
                lhsT=w_words[:, a, 2 * m * P : 2 * (m + 1) * P].bitcast(FP4X4),
                lhsT_scale=w_plane[:, a, m * P : (m + 1) * P],
                rhs=words[:, a, 2 * b0 * TB : 2 * (b0 + 1) * TB].bitcast(FP4X4),
                rhs_scale=x_plane[:, a, b * TB : (b + 1) * TB],
                start=(a == 0),
                stop=False,
            )

        def xr_pass(i, a, m, b):
            nc.tensor.matmul_mx(
                out=banks[i][:],
                lhsT=w_words[:, a, 2 * m * P : 2 * (m + 1) * P].bitcast(FP4X4),
                lhsT_scale=w_plane[:, a, m * P : (m + 1) * P],
                rhs=codes[a, b][:].bitcast(FP8X4),
                rhs_scale=scales[a, b][:],
                start=False,
                stop=(a == A - 1),
            )

        held = {}

        def hold(engine_copy, i, m, b):
            y = keep.tile([P, TB], F32, name="y%d_%d" % (m, b))
            engine_copy(out=y[:], in_=banks[i][:])
            held[m, b] = y

        def finish(i, m, b):
            gm = g_tiles[m // 2][:, m % 2, b * TB : (b + 1) * TB]
            y = held[m, b] if (m, b) in held else banks[i]
            nc.vector.tensor_mul(out=gm, in0=y[:], in1=gm)

        def store(m, c0, c1):
            queue = nc.sync if m % 2 == 0 else nc.scalar
            queue.dma_start(out=out[m * P : (m + 1) * P, c0:c1], in_=g_tiles[m // 2][:, m % 2, c0:c1])

        for m in range(MT):
            open_bank(m)
        for a in range(A):
            for m in range(MT):
                x4_pass(m, a, m, 0)
        for a in range(A):
            quantise(a, 0)
            for m in range(MT):
                xr_pass(m, a, m, 0)
        half = [(m, b) for m in range(MT // 2) for b in (1, 2)]
        for i, (m, b) in enumerate(half):
            hold(nc.scalar.copy if i % 2 == 0 else nc.vector.tensor_copy, i, i, 0)
            open_bank(i)
            for a in range(A):
                x4_pass(i, a, m, b)
        for a in (0, 1):
            quantise(a, 1)
            quantise(a, 2)
        quantise(2, 1)
        quantise(2, 2)
        for a in range(A):
            for i, (m, b) in enumerate(half):
                xr_pass(i, a, m, b)
        for i, (m, b) in enumerate(half):
            hold(nc.scalar.copy, i, m, b)
            open_bank(i)
            for a in range(A):
                x4_pass(i, a, m + MT // 2, b)
            for a in range(A):
                xr_pass(i, a, m + MT // 2, b)
        for m in range(MT):
            finish(0, m, 0)
            for b in (1, 2):
                finish(2 * (m % (MT // 2)) + b - 1, m, b)
                if m == MT - 1:
                    store(m, (b - 1) * 2 * TB, (b + 1) * TB)
            if m < MT - 1:
                store(m, 0, T)
